import numpy as np
import ml_dtypes


def mxq(x, axis, fmt="e4m3"):
    dtype, down = {"e4m3": (ml_dtypes.float8_e4m3fn, 7), "e5m2": (ml_dtypes.float8_e5m2, 14)}[fmt]
    v = np.moveaxis(np.asarray(x, np.float32).astype(ml_dtypes.bfloat16).astype(np.float64), axis, -1)
    blocks = v.reshape(v.shape[:-1] + (-1, 32))
    amax = np.abs(blocks).max(-1, keepdims=True)
    byte = np.maximum(np.where(amax > 0, np.frexp(amax)[1] - 1 + 127, 0) - down, 1)
    scale = np.exp2(byte - 127.0)
    codes = (blocks / scale).astype(np.float32).astype(dtype).astype(np.float64)
    return np.moveaxis((codes * scale).reshape(v.shape), -1, axis)


WIDE = False


def mx_kscale(k):
    if not WIDE:
        return np.ones(k)
    levels = np.array([10, -10, 5, -5, 0])
    if k % 512:
        return np.exp2(np.random.permutation(np.resize(levels, k // 32))).repeat(32)
    a = np.empty((k // 512, 16))
    for p in range(k // 512):
        a[p, :8] = np.random.permutation(np.resize(levels, 8))
        for g in range(8):
            far = levels[np.abs(levels - a[p, g]) >= 10]
            a[p, g + 8] = far[np.random.randint(len(far))]
    return np.exp2(a.ravel()).repeat(32)


def f64(x):
    return np.asarray(x).astype(np.float64)


def striped(idx):
    return np.tile(np.asarray(idx).reshape(-1, 16).T, (8, 1)).astype(np.uint16)


def unstriped(offs):
    return offs[:16].T.reshape(-1).astype(np.int64)


E2M1 = np.array([0.0, 0.5, 1.0, 1.5, 2.0, 3.0, 4.0, 6.0, -0.0, -0.5, -1.0, -1.5, -2.0, -3.0, -4.0, -6.0])


def pack_weight(w, fmt):
    k, n = w.shape
    w = f64(np.asarray(w, np.float32).astype(ml_dtypes.bfloat16)).reshape(k // 32, 32, n)
    amax = np.abs(w).max(1)
    if fmt == "e4m3":
        byte = np.frexp(amax)[1] - 1 + 127 - 7
    else:
        mant, ex = np.frexp(amax / 6.0)
        byte = np.where(mant > 0.5, ex, ex - 1) + 127
    byte = np.clip(np.where(amax > 0, byte, 1), 1, 254)
    scaled = (w * np.exp2(127.0 - byte)[:, None, :]).reshape(k, n).astype(np.float32)
    by_word = np.ascontiguousarray(scaled.reshape(k // 512, 128, 4, n).transpose(0, 1, 3, 2))
    if fmt == "e4m3":
        words = by_word.astype(ml_dtypes.float8_e4m3fn).view(np.uint8)
    else:
        c = by_word.astype(ml_dtypes.float4_e2m1fn).view(np.uint8) & 0xF
        words = (c[..., 0::2] | (c[..., 1::2] << 4)).reshape(k // 512, 128, 2 * n)
    return np.ascontiguousarray(words), np.ascontiguousarray(byte.astype(np.uint8).reshape(k // 512, 16, n))


def unpack_weight(words, scales, fmt):
    g, _, n = scales.shape
    words = np.ascontiguousarray(words).reshape(g, 128, n, -1)
    if fmt == "e4m3":
        vals = words.view(ml_dtypes.float8_e4m3fn).astype(np.float64)
    else:
        nib = np.empty((g, 128, n, 4), np.uint8)
        nib[..., 0::2] = words & 0xF
        nib[..., 1::2] = words >> 4
        vals = E2M1[nib]
    vals = vals * np.repeat(np.exp2(scales.astype(np.float64) - 127.0), 8, axis=1)[..., None]
    return vals.transpose(0, 1, 3, 2).reshape(g * 512, n)


def sigmoid(v):
    return 1.0 / (1.0 + np.exp(-v))


D, K, R, T, I, Q, U = 512, 512, 512, 2048, 512, 128, 1024


def setup_inputs():
    n = np.random.standard_normal
    idx2 = np.random.permutation(U)[:I]
    idx = np.random.permutation(T)[:I]
    fd = mx_kscale(D)
    fk = mx_kscale(K)
    fr = mx_kscale(R)
    keysp = pack_weight(n((D, T)) / fd[:, None], "e4m3")
    tabp = pack_weight(n((K, T)) / fk[:, None], "e4m3")
    return {
        "query": (n((D, Q)) * 0.7 / np.sqrt(D) * fd[:, None]).astype(np.float32),
        "keys_words": keysp[0],
        "keys_scales": keysp[1],
        "tab_words": tabp[0],
        "tab_scales": tabp[1],
        "w1": (n((K, R)) * 1 / np.sqrt(K) * fk[:, None]).astype(np.float32),
        "gtab": (n((R, U))).astype(np.float32),
        "gout": (n((R, Q)) * 1 / np.sqrt(R) * fr[:, None]).astype(np.float32),
        "hsc": (np.random.uniform(0.7, 1.4, (R, 1)) / fr[:, None]).astype(np.float32),
        "old": (0.5 * n((Q, T))).astype(np.float32),
        "offs2": striped(idx2),
        "offs": striped(idx),
    }


def reference(query, keys_words, keys_scales, tab_words, tab_scales, w1, gtab, gout, hsc, old, offs2, offs):
    idx2 = unstriped(offs2)
    idx = unstriped(offs)
    keysu = unpack_weight(keys_words, keys_scales, "e4m3")
    tabu = unpack_weight(tab_words, tab_scales, "e4m3")
    queryq = mxq(f64(query), 0, "e4m3")
    keysidxg = keysu[:, idx]
    a = queryq.T @ keysidxg
    p = np.exp(a - np.max(a, axis=1, keepdims=True))
    z = np.sum(p, axis=1, keepdims=True)
    w1q = mxq(f64(w1), 0, "e4m3")
    tabidxg = tabu[:, idx]
    zh = w1q.T @ tabidxg
    hg = sigmoid(f64(gtab)[:, idx2])
    hv = zh * hg
    hs1 = hv * f64(hsc)
    goutq = mxq(f64(gout), 0, "e4m3")
    hs1q = mxq(hs1, 0, "e4m3")
    c0 = goutq.T @ hs1q
    dz = np.sum(c0 * p / np.square(z) * (-1.0), axis=1, keepdims=True)
    dp = c0 / z + dz
    da = dp * p
    gs = da * 512.0
    gf = np.zeros((Q, T))
    gf[:, idx] = gs
    y = f64(old) + gf
    return y

@@ -1,0 +1,189 @@
+from contextlib import ExitStack
+
+import concourse.mybir as mybir
+
+F32 = mybir.dt.float32
+BF16 = mybir.dt.bfloat16
+I32 = mybir.dt.int32
+U32 = mybir.dt.uint32
+U16 = mybir.dt.uint16
+U8 = mybir.dt.uint8
+FP8X4 = mybir.dt.float8_e4m3fn_x4
+ACT = mybir.ActivationFunctionType
+ALU = mybir.AluOpType
+AXIS = mybir.AxisListType
+
+P = 128
+PACK = 4
+D, K, R, T, SLOTS, Q, U = 512, 512, 512, 2048, 512, 128, 1024
+CHUNK = 128
+CHUNKS = SLOTS // CHUNK
+STORE_WIDTHS = (256, 512, 512, 512, 256)
+
+FLOPS = 2 * SLOTS * (D * Q + K * R + R * Q)
+
+
+def tile_attend_blrgated_soft_kernel(tc, query, keys_words, keys_scales, tab_words, tab_scales, w1, gtab, gout, hsc, old, offs2, offs, out):
+    nc = tc.nc
+    with ExitStack() as ctx:
+        pool = ctx.enter_context(tc.tile_pool(name="pool", bufs=1))
+        psum = ctx.enter_context(tc.psum_pool(name="psum", bufs=1))
+
+        def tile(name, shape, dtype):
+            return pool.tile(shape, dtype, name=name, align_bytes=64)
+
+        gate_list = pool.tile([P, SLOTS // 16], U16, name="gate_list")
+        token_list = pool.tile([P, SLOTS // 16], U16, name="token_list")
+        tab_pool_s = tile("tab_pool_s", [P, T], U8)
+        keys_pool_s = tile("keys_pool_s", [P, T], U8)
+        tab_pool_w = tile("tab_pool_w", [P, T], U32)
+        keys_pool_w = tile("keys_pool_w", [P, T], U32)
+        gate_pool = [tile(f"gate_pool{j}", [P, U], F32) for j in range(PACK)]
+        w1_raw = tile("w1_raw", [P, PACK, R], F32)
+        query_raw = tile("query_raw", [P, PACK, Q], F32)
+        gout_raw = tile("gout_raw", [P, PACK, Q], F32)
+        hsc_cols = tile("hsc_cols", [P, PACK], F32)
+        old_rows = tile("old_rows", [P, T], F32)
+        placed = tile("placed", [P, T], F32)
+
+        nc.vector.memset(keys_pool_s[:].bitcast(I32), 0)
+        nc.vector.memset(tab_pool_s[:].bitcast(I32), 0)
+        nc.vector.memset(placed[:], 0.0)
+
+        def load_words(dst, words):
+            nc.sync.dma_start(dst[:].bitcast(I32), words[0].rearrange("p n t -> p (n t)").bitcast(I32))
+
+        def load_scales(queue, dst, scales):
+            for quad in range(4):
+                queue.dma_start(dst[32 * quad : 32 * quad + 4, :].bitcast(I32), scales[0, 4 * quad : 4 * quad + 4, :].bitcast(I32))
+
+        gtab_planes = gtab.rearrange("(p j) u -> p j u", j=PACK)
+
+        def load_gates(j):
+            nc.sync.dma_start(gate_pool[j][:], gtab_planes[:, j, :])
+
+        nc.sync.dma_start(gate_list[:], offs2)
+        load_gates(0)
+        nc.sync.dma_start(token_list[:], offs)
+        load_scales(nc.sync, keys_pool_s, keys_scales)
+        load_gates(1)
+        nc.sync.dma_start(w1_raw[:], w1.rearrange("(p j) c -> p j c", j=PACK))
+        nc.sync.dma_start(hsc_cols[:], hsc.rearrange("(p j) o -> p (j o)", j=PACK))
+        load_scales(nc.sync, tab_pool_s, tab_scales)
+        load_gates(2)
+        load_words(tab_pool_w, tab_words)
+        load_gates(3)
+        nc.sync.dma_start(query_raw[:], query.rearrange("(p j) c -> p j c", j=PACK))
+        load_words(keys_pool_w, keys_words)
+        nc.sync.dma_start(gout_raw[:], gout.rearrange("(p j) c -> p j c", j=PACK))
+        nc.sync.dma_start(old_rows[:], old)
+
+        warm = [tile(f"warm{n}", [P, 1], F32) for n in range(2)]
+        nc.scalar.activation(warm[0][:], placed[:, 0:1], ACT.Sigmoid)
+
+        gates = [tile(f"gates{j}", [P, SLOTS], F32) for j in range(PACK)]
+        factor = tile("factor", [P, SLOTS // 4, PACK, 4], F32)
+        for j in range(PACK):
+            pieces = CHUNKS if j == PACK - 1 else 1
+            width = SLOTS // pieces
+            for s in range(0, SLOTS, width):
+                nc.scalar.activation(gates[j][:, s : s + width], gate_pool[j][:].indirect(gate_list[:, s // 16 : (s + width) // 16]), ACT.Sigmoid)
+                nc.scalar.activation(factor[:, s // 4 : (s + width) // 4, j, :], gates[j][:, s : s + width].rearrange("p (c i) -> p c i", i=4), ACT.Copy, scale=hsc_cols[:, j : j + 1])
+        nc.scalar.activation(warm[1][:], gates[PACK - 1][:, SLOTS - 1 : SLOTS], ACT.Exp)
+
+        tab_s = tile("tab_s", [P, SLOTS], U8)
+        keys_s = tile("keys_s", [P, SLOTS], U8)
+        tab_w = tile("tab_w", [P, SLOTS], U32)
+        keys_w = tile("keys_w", [P, SLOTS], U32)
+        nc.vector.tensor_copy(keys_s[:], keys_pool_s[:].indirect(token_list[:]))
+
+        w1_bf = tile("w1_bf", [P, PACK, P, PACK], BF16)
+        w1_w = tile("w1_w", [P, R], U32)
+        w1_s = tile("w1_s", [P, R], U8)
+        nc.vector.tensor_copy(w1_bf[:].rearrange("p t m j -> p m j t"), w1_raw[:].rearrange("p j (m t) -> p m j t", t=PACK))
+        nc.vector.tensor_copy(tab_s[:], tab_pool_s[:].indirect(token_list[:]))
+        nc.vector.quantize_mx(w1_w[:].bitcast(FP8X4), w1_s[:], w1_bf[:].rearrange("p t m j -> p (t m j)"))
+
+        def small_operand(name, raw):
+            bf = tile(name + "_bf", [P, Q, PACK], BF16)
+            words = tile(name + "_w", [P, Q], U32)
+            scales = tile(name + "_s", [P, Q], U8)
+            nc.scalar.copy(bf[:].rearrange("p (c i) j -> p c j i", i=4), raw[:].rearrange("p j (c i) -> p c j i", i=4))
+            return bf, words, scales
+
+        def quantize(words, scales, bf):
+            nc.vector.quantize_mx(words.bitcast(FP8X4), scales, bf.rearrange("p n j -> p (n j)"))
+
+        query_bf, query_w, query_s = small_operand("query", query_raw)
+        gout_bf, gout_w, gout_s = small_operand("gout", gout_raw)
+
+        half = SLOTS // 2
+        for h in range(2):
+            nc.vector.tensor_copy(tab_w[:, h * half : (h + 1) * half], tab_pool_w[:].indirect(token_list[:, h * half // 16 : (h + 1) * half // 16]))
+
+        zh = [psum.tile([P, PACK, CHUNK], F32, name=f"zh{c}") for c in range(CHUNKS)]
+        c0 = psum.tile([P, SLOTS], F32, name="c0")
+        scores = psum.tile([P, SLOTS], F32, name="scores")
+        hs_bf = [tile(f"hs_bf{c}", [P, CHUNK, PACK], BF16) for c in range(CHUNKS)]
+        hs_w = [tile(f"hs_w{c}", [P, CHUNK], U32) for c in range(CHUNKS)]
+        hs_s = [tile(f"hs_s{c}", [P, CHUNK], U8) for c in range(CHUNKS)]
+
+        def layer(c):
+            cols = slice(c * CHUNK, (c + 1) * CHUNK)
+            for t in range(PACK):
+                feats = slice(t * P, (t + 1) * P)
+                nc.tensor.matmul_mx(zh[c][:, t, :], w1_w[:, feats].bitcast(FP8X4), w1_s[:, feats], tab_w[:, cols].bitcast(FP8X4), tab_s[:, cols], start=True, stop=True)
+
+        def gate(c):
+            nc.vector.tensor_tensor(
+                hs_bf[c][:].rearrange("p (c i) t -> p c t i", i=4),
+                zh[c][:].rearrange("p t (c i) -> p c t i", i=4),
+                factor[:, c * CHUNK // 4 : (c + 1) * CHUNK // 4, :, :],
+                ALU.mult,
+            )
+
+        def quantize_hs(c):
+            quantize(hs_w[c][:], hs_s[c][:], hs_bf[c][:])
+
+        def read_back(c):
+            nc.tensor.matmul_mx(c0[:, c * CHUNK : (c + 1) * CHUNK], gout_w[:].bitcast(FP8X4), gout_s[:], hs_w[c][:].bitcast(FP8X4), hs_s[c][:], start=True, stop=True)
+
+        stats = [tile(f"stat{n}", [P, 1], F32) for n in range(5)]
+        neg_max, z, inv_z, inv_z512, mean = stats
+        p = tile("p", [P, SLOTS], F32)
+        weighted = tile("weighted", [P, SLOTS], F32)
+        centred = tile("centred", [P, SLOTS], F32)
+
+        for c in range(CHUNKS):
+            layer(c)
+        gate(0)
+        gate(1)
+        quantize(query_w[:], query_s[:], query_bf[:])
+        quantize_hs(0)
+        gate(2)
+        quantize_hs(1)
+        nc.vector.tensor_copy(keys_w[:], keys_pool_w[:].indirect(token_list[:]))
+        nc.tensor.matmul_mx(scores[:], query_w[:].bitcast(FP8X4), query_s[:], keys_w[:].bitcast(FP8X4), keys_s[:], start=True, stop=True)
+        gate(3)
+        nc.vector.tensor_reduce(neg_max[:], scores[:], AXIS.X, ALU.max, negate=True)
+        nc.scalar.activation(p[:], scores[:], ACT.Exp, bias=neg_max[:], accum_out=z[:])
+        quantize(gout_w[:], gout_s[:], gout_bf[:])
+        quantize_hs(2)
+        quantize_hs(3)
+        for c in range(CHUNKS):
+            read_back(c)
+
+        nc.vector.reciprocal(inv_z[:], z[:])
+        nc.vector.scalar_tensor_tensor(weighted[:], c0[:], inv_z[:], p[:], ALU.mult, ALU.mult, accum_out=mean[:])
+        nc.vector.tensor_scalar(inv_z512[:], inv_z[:], 512.0, None, ALU.mult)
+        nc.vector.tensor_scalar(centred[:], c0[:], mean[:], inv_z512[:], ALU.subtract, ALU.mult)
+        nc.vector.tensor_tensor(placed[:].indirect(token_list[:]), centred[:], p[:], ALU.mult)
+
+        start = 0
+        for n, width in enumerate(STORE_WIDTHS):
+            cols = slice(start, start + width)
+            total = tile(f"total{n}", [P, width], F32)
+            nc.vector.tensor_tensor(total[:], placed[:, cols], old_rows[:, cols], ALU.add)
+            queue = nc.sync if n % 2 == 0 else nc.scalar
+            queue.dma_start(out[:, cols], total[:])
+            start = start + width

@@ -18,6 +18,9 @@ PACK = 4
 D, K, R, T, SLOTS, Q, U = 512, 512, 512, 2048, 512, 128, 1024
 CHUNK = 128
 CHUNKS = SLOTS // CHUNK
+KEYS_ROW, TAB_ROW = 8, 12
+VECTOR_PLANES = (1,)
+HELD = 2
 STORE_WIDTHS = (256, 512, 512, 512, 256)
 
 FLOPS = 2 * SLOTS * (D * Q + K * R + R * Q)
@@ -49,13 +52,17 @@ def tile_attend_blrgated_soft_kernel(tc, query, keys_words, keys_scales, tab_wor
         nc.vector.memset(keys_pool_s[:].bitcast(I32), 0)
         nc.vector.memset(tab_pool_s[:].bitcast(I32), 0)
         nc.vector.memset(placed[:], 0.0)
+        consts = tile("consts", [P, 2], F32)
+        nc.vector.memset(consts[:, 0:1], 512.0)
+        nc.vector.memset(consts[:, 1:2], -1.0)
 
         def load_words(dst, words):
             nc.sync.dma_start(dst[:].bitcast(I32), words[0].rearrange("p n t -> p (n t)").bitcast(I32))
 
-        def load_scales(queue, dst, scales):
-            for quad in range(4):
-                queue.dma_start(dst[32 * quad : 32 * quad + 4, :].bitcast(I32), scales[0, 4 * quad : 4 * quad + 4, :].bitcast(I32))
+        def load_scales(dst, first, scales):
+            rows = scales[0].rearrange("(quad r) n -> r quad n", r=4)
+            for r in range(4):
+                nc.sync.dma_start(dst[first + r : P : 32, :].bitcast(I32), rows[r].bitcast(I32))
 
         gtab_planes = gtab.rearrange("(p j) u -> p j u", j=PACK)
 
@@ -65,11 +72,11 @@ def tile_attend_blrgated_soft_kernel(tc, query, keys_words, keys_scales, tab_wor
         nc.sync.dma_start(gate_list[:], offs2)
         load_gates(0)
         nc.sync.dma_start(token_list[:], offs)
-        load_scales(nc.sync, keys_pool_s, keys_scales)
-        load_gates(1)
+        load_scales(keys_pool_s, KEYS_ROW, keys_scales)
         nc.sync.dma_start(w1_raw[:], w1.rearrange("(p j) c -> p j c", j=PACK))
         nc.sync.dma_start(hsc_cols[:], hsc.rearrange("(p j) o -> p (j o)", j=PACK))
-        load_scales(nc.sync, tab_pool_s, tab_scales)
+        load_scales(tab_pool_s, TAB_ROW, tab_scales)
+        load_gates(1)
         load_gates(2)
         load_words(tab_pool_w, tab_words)
         load_gates(3)
@@ -88,8 +95,8 @@ def tile_attend_blrgated_soft_kernel(tc, query, keys_words, keys_scales, tab_wor
             width = SLOTS // pieces
             for s in range(0, SLOTS, width):
                 nc.scalar.activation(gates[j][:, s : s + width], gate_pool[j][:].indirect(gate_list[:, s // 16 : (s + width) // 16]), ACT.Sigmoid)
-                nc.scalar.activation(factor[:, s // 4 : (s + width) // 4, j, :], gates[j][:, s : s + width].rearrange("p (c i) -> p c i", i=4), ACT.Copy, scale=hsc_cols[:, j : j + 1])
-        nc.scalar.activation(warm[1][:], gates[PACK - 1][:, SLOTS - 1 : SLOTS], ACT.Exp)
+                if j not in VECTOR_PLANES:
+                    nc.scalar.activation(factor[:, s // 4 : (s + width) // 4, j, :], gates[j][:, s : s + width].rearrange("p (c i) -> p c i", i=4), ACT.Copy, scale=hsc_cols[:, j : j + 1])
 
         tab_s = tile("tab_s", [P, SLOTS], U8)
         keys_s = tile("keys_s", [P, SLOTS], U8)
@@ -103,6 +110,8 @@ def tile_attend_blrgated_soft_kernel(tc, query, keys_words, keys_scales, tab_wor
         nc.vector.tensor_copy(w1_bf[:].rearrange("p t m j -> p m j t"), w1_raw[:].rearrange("p j (m t) -> p m j t", t=PACK))
         nc.vector.tensor_copy(tab_s[:], tab_pool_s[:].indirect(token_list[:]))
         nc.vector.quantize_mx(w1_w[:].bitcast(FP8X4), w1_s[:], w1_bf[:].rearrange("p t m j -> p (t m j)"))
+        for j in VECTOR_PLANES:
+            nc.vector.tensor_scalar(factor[:, :, j, :], gates[j][:].rearrange("p (c i) -> p c i", i=4), hsc_cols[:, j : j + 1], None, ALU.mult)
 
         def small_operand(name, raw):
             bf = tile(name + "_bf", [P, Q, PACK], BF16)
@@ -115,6 +124,7 @@ def tile_attend_blrgated_soft_kernel(tc, query, keys_words, keys_scales, tab_wor
             nc.vector.quantize_mx(words.bitcast(FP8X4), scales, bf.rearrange("p n j -> p (n j)"))
 
         query_bf, query_w, query_s = small_operand("query", query_raw)
+        nc.scalar.activation(warm[1][:], factor[:, SLOTS // 4 - 1, PACK - 1, 0:1], ACT.Exp, scale=0.0)
         gout_bf, gout_w, gout_s = small_operand("gout", gout_raw)
 
         half = SLOTS // 2
@@ -124,7 +134,7 @@ def tile_attend_blrgated_soft_kernel(tc, query, keys_words, keys_scales, tab_wor
         zh = [psum.tile([P, PACK, CHUNK], F32, name=f"zh{c}") for c in range(CHUNKS)]
         c0 = psum.tile([P, SLOTS], F32, name="c0")
         scores = psum.tile([P, SLOTS], F32, name="scores")
-        hs_bf = [tile(f"hs_bf{c}", [P, CHUNK, PACK], BF16) for c in range(CHUNKS)]
+        hs_bf = [tile(f"hs_bf{c}", [P, CHUNK, PACK], BF16)[:] for c in range(HELD)]
         hs_w = [tile(f"hs_w{c}", [P, CHUNK], U32) for c in range(CHUNKS)]
         hs_s = [tile(f"hs_s{c}", [P, CHUNK], U8) for c in range(CHUNKS)]
 
@@ -132,41 +142,43 @@ def tile_attend_blrgated_soft_kernel(tc, query, keys_words, keys_scales, tab_wor
             cols = slice(c * CHUNK, (c + 1) * CHUNK)
             for t in range(PACK):
                 feats = slice(t * P, (t + 1) * P)
-                nc.tensor.matmul_mx(zh[c][:, t, :], w1_w[:, feats].bitcast(FP8X4), w1_s[:, feats], tab_w[:, cols].bitcast(FP8X4), tab_s[:, cols], start=True, stop=True)
+                nc.tensor.matmul_mx(zh[c][:, t, :], w1_w[:, feats].bitcast(FP8X4), w1_s[:, feats], tab_w[:, cols].bitcast(FP8X4), tab_s[TAB_ROW:P, cols], start=True, stop=True)
 
         def gate(c):
             nc.vector.tensor_tensor(
-                hs_bf[c][:].rearrange("p (c i) t -> p c t i", i=4),
+                hs_bf[c].rearrange("p (c i) t -> p c t i", i=4),
                 zh[c][:].rearrange("p t (c i) -> p c t i", i=4),
                 factor[:, c * CHUNK // 4 : (c + 1) * CHUNK // 4, :, :],
                 ALU.mult,
             )
 
         def quantize_hs(c):
-            quantize(hs_w[c][:], hs_s[c][:], hs_bf[c][:])
+            quantize(hs_w[c][:], hs_s[c][:], hs_bf[c])
 
         def read_back(c):
             nc.tensor.matmul_mx(c0[:, c * CHUNK : (c + 1) * CHUNK], gout_w[:].bitcast(FP8X4), gout_s[:], hs_w[c][:].bitcast(FP8X4), hs_s[c][:], start=True, stop=True)
 
-        stats = [tile(f"stat{n}", [P, 1], F32) for n in range(5)]
-        neg_max, z, inv_z, inv_z512, mean = stats
+        neg_max, z, inv_z, total512 = [tile(f"stat{n}", [P, 1], F32) for n in range(4)]
         p = tile("p", [P, SLOTS], F32)
         weighted = tile("weighted", [P, SLOTS], F32)
-        centred = tile("centred", [P, SLOTS], F32)
+        shift = tile("shift", [P, SLOTS], F32)
+        inv_pair = tile("inv_pair", [P, 2], F32)
 
         for c in range(CHUNKS):
             layer(c)
         gate(0)
         gate(1)
-        quantize(query_w[:], query_s[:], query_bf[:])
         quantize_hs(0)
-        gate(2)
+        quantize(query_w[:], query_s[:], query_bf[:])
         quantize_hs(1)
         nc.vector.tensor_copy(keys_w[:], keys_pool_w[:].indirect(token_list[:]))
-        nc.tensor.matmul_mx(scores[:], query_w[:].bitcast(FP8X4), query_s[:], keys_w[:].bitcast(FP8X4), keys_s[:], start=True, stop=True)
-        gate(3)
+        nc.tensor.matmul_mx(scores[:], query_w[:].bitcast(FP8X4), query_s[:], keys_w[:].bitcast(FP8X4), keys_s[KEYS_ROW:P, :], start=True, stop=True)
+        held = pool.tile([P, 2, CHUNK, PACK], BF16, name="hs_held", tag="keys_pool_w", align_bytes=64)
+        hs_bf.extend(held[:, c] for c in range(CHUNKS - HELD))
+        gate(2)
         nc.vector.tensor_reduce(neg_max[:], scores[:], AXIS.X, ALU.max, negate=True)
         nc.scalar.activation(p[:], scores[:], ACT.Exp, bias=neg_max[:], accum_out=z[:])
+        gate(3)
         quantize(gout_w[:], gout_s[:], gout_bf[:])
         quantize_hs(2)
         quantize_hs(3)
@@ -174,10 +186,10 @@ def tile_attend_blrgated_soft_kernel(tc, query, keys_words, keys_scales, tab_wor
             read_back(c)
 
         nc.vector.reciprocal(inv_z[:], z[:])
-        nc.vector.scalar_tensor_tensor(weighted[:], c0[:], inv_z[:], p[:], ALU.mult, ALU.mult, accum_out=mean[:])
-        nc.vector.tensor_scalar(inv_z512[:], inv_z[:], 512.0, None, ALU.mult)
-        nc.vector.tensor_scalar(centred[:], c0[:], mean[:], inv_z512[:], ALU.subtract, ALU.mult)
-        nc.vector.tensor_tensor(placed[:].indirect(token_list[:]), centred[:], p[:], ALU.mult)
+        nc.vector.tensor_scalar(inv_pair[:], consts[:], inv_z[:], None, ALU.mult)
+        nc.vector.scalar_tensor_tensor(weighted[:], c0[:], inv_pair[:, 0:1], p[:], ALU.mult, ALU.mult, accum_out=total512[:])
+        nc.vector.tensor_scalar(shift[:], p[:], total512[:], inv_pair[:, 1:2], ALU.mult, ALU.mult)
+        nc.vector.tensor_tensor(placed[:].indirect(token_list[:]), weighted[:], shift[:], ALU.add)
 
         start = 0
         for n, width in enumerate(STORE_WIDTHS):

from contextlib import ExitStack

import concourse.mybir as mybir

F32 = mybir.dt.float32
BF16 = mybir.dt.bfloat16
I32 = mybir.dt.int32
U32 = mybir.dt.uint32
U16 = mybir.dt.uint16
U8 = mybir.dt.uint8
FP8X4 = mybir.dt.float8_e4m3fn_x4
ACT = mybir.ActivationFunctionType
ALU = mybir.AluOpType
AXIS = mybir.AxisListType

P = 128
PACK = 4
D, K, R, T, SLOTS, Q, U = 512, 512, 512, 2048, 512, 128, 1024
CHUNK = 128
CHUNKS = SLOTS // CHUNK
KEYS_ROW, TAB_ROW = 8, 12
VECTOR_PLANES = (1,)
HELD = 2
STORE_WIDTHS = (256, 512, 512, 512, 256)

FLOPS = 2 * SLOTS * (D * Q + K * R + R * Q)


def tile_attend_blrgated_soft_kernel(tc, query, keys_words, keys_scales, tab_words, tab_scales, w1, gtab, gout, hsc, old, offs2, offs, out):
    nc = tc.nc
    with ExitStack() as ctx:
        pool = ctx.enter_context(tc.tile_pool(name="pool", bufs=1))
        psum = ctx.enter_context(tc.psum_pool(name="psum", bufs=1))

        def tile(name, shape, dtype):
            return pool.tile(shape, dtype, name=name, align_bytes=64)

        gate_list = pool.tile([P, SLOTS // 16], U16, name="gate_list")
        token_list = pool.tile([P, SLOTS // 16], U16, name="token_list")
        tab_pool_s = tile("tab_pool_s", [P, T], U8)
        keys_pool_s = tile("keys_pool_s", [P, T], U8)
        tab_pool_w = tile("tab_pool_w", [P, T], U32)
        keys_pool_w = tile("keys_pool_w", [P, T], U32)
        gate_pool = [tile(f"gate_pool{j}", [P, U], F32) for j in range(PACK)]
        w1_raw = tile("w1_raw", [P, PACK, R], F32)
        query_raw = tile("query_raw", [P, PACK, Q], F32)
        gout_raw = tile("gout_raw", [P, PACK, Q], F32)
        hsc_cols = tile("hsc_cols", [P, PACK], F32)
        old_rows = tile("old_rows", [P, T], F32)
        placed = tile("placed", [P, T], F32)

        nc.vector.memset(keys_pool_s[:].bitcast(I32), 0)
        nc.vector.memset(tab_pool_s[:].bitcast(I32), 0)
        nc.vector.memset(placed[:], 0.0)
        consts = tile("consts", [P, 2], F32)
        nc.vector.memset(consts[:, 0:1], 512.0)
        nc.vector.memset(consts[:, 1:2], -1.0)

        def load_words(dst, words):
            nc.sync.dma_start(dst[:].bitcast(I32), words[0].rearrange("p n t -> p (n t)").bitcast(I32))

        def load_scales(dst, first, scales):
            rows = scales[0].rearrange("(quad r) n -> r quad n", r=4)
            for r in range(4):
                nc.sync.dma_start(dst[first + r : P : 32, :].bitcast(I32), rows[r].bitcast(I32))

        gtab_planes = gtab.rearrange("(p j) u -> p j u", j=PACK)

        def load_gates(j):
            nc.sync.dma_start(gate_pool[j][:], gtab_planes[:, j, :])

        nc.sync.dma_start(gate_list[:], offs2)
        load_gates(0)
        nc.sync.dma_start(token_list[:], offs)
        load_scales(keys_pool_s, KEYS_ROW, keys_scales)
        nc.sync.dma_start(w1_raw[:], w1.rearrange("(p j) c -> p j c", j=PACK))
        nc.sync.dma_start(hsc_cols[:], hsc.rearrange("(p j) o -> p (j o)", j=PACK))
        load_scales(tab_pool_s, TAB_ROW, tab_scales)
        load_gates(1)
        load_gates(2)
        load_words(tab_pool_w, tab_words)
        load_gates(3)
        nc.sync.dma_start(query_raw[:], query.rearrange("(p j) c -> p j c", j=PACK))
        load_words(keys_pool_w, keys_words)
        nc.sync.dma_start(gout_raw[:], gout.rearrange("(p j) c -> p j c", j=PACK))
        nc.sync.dma_start(old_rows[:], old)

        warm = [tile(f"warm{n}", [P, 1], F32) for n in range(2)]
        nc.scalar.activation(warm[0][:], placed[:, 0:1], ACT.Sigmoid)

        gates = [tile(f"gates{j}", [P, SLOTS], F32) for j in range(PACK)]
        factor = tile("factor", [P, SLOTS // 4, PACK, 4], F32)
        for j in range(PACK):
            pieces = CHUNKS if j == PACK - 1 else 1
            width = SLOTS // pieces
            for s in range(0, SLOTS, width):
                nc.scalar.activation(gates[j][:, s : s + width], gate_pool[j][:].indirect(gate_list[:, s // 16 : (s + width) // 16]), ACT.Sigmoid)
                if j not in VECTOR_PLANES:
                    nc.scalar.activation(factor[:, s // 4 : (s + width) // 4, j, :], gates[j][:, s : s + width].rearrange("p (c i) -> p c i", i=4), ACT.Copy, scale=hsc_cols[:, j : j + 1])

        tab_s = tile("tab_s", [P, SLOTS], U8)
        keys_s = tile("keys_s", [P, SLOTS], U8)
        tab_w = tile("tab_w", [P, SLOTS], U32)
        keys_w = tile("keys_w", [P, SLOTS], U32)
        nc.vector.tensor_copy(keys_s[:], keys_pool_s[:].indirect(token_list[:]))

        w1_bf = tile("w1_bf", [P, PACK, P, PACK], BF16)
        w1_w = tile("w1_w", [P, R], U32)
        w1_s = tile("w1_s", [P, R], U8)
        nc.vector.tensor_copy(w1_bf[:].rearrange("p t m j -> p m j t"), w1_raw[:].rearrange("p j (m t) -> p m j t", t=PACK))
        nc.vector.tensor_copy(tab_s[:], tab_pool_s[:].indirect(token_list[:]))
        nc.vector.quantize_mx(w1_w[:].bitcast(FP8X4), w1_s[:], w1_bf[:].rearrange("p t m j -> p (t m j)"))
        for j in VECTOR_PLANES:
            nc.vector.tensor_scalar(factor[:, :, j, :], gates[j][:].rearrange("p (c i) -> p c i", i=4), hsc_cols[:, j : j + 1], None, ALU.mult)

        def small_operand(name, raw):
            bf = tile(name + "_bf", [P, Q, PACK], BF16)
            words = tile(name + "_w", [P, Q], U32)
            scales = tile(name + "_s", [P, Q], U8)
            nc.scalar.copy(bf[:].rearrange("p (c i) j -> p c j i", i=4), raw[:].rearrange("p j (c i) -> p c j i", i=4))
            return bf, words, scales

        def quantize(words, scales, bf):
            nc.vector.quantize_mx(words.bitcast(FP8X4), scales, bf.rearrange("p n j -> p (n j)"))

        query_bf, query_w, query_s = small_operand("query", query_raw)
        nc.scalar.activation(warm[1][:], factor[:, SLOTS // 4 - 1, PACK - 1, 0:1], ACT.Exp, scale=0.0)
        gout_bf, gout_w, gout_s = small_operand("gout", gout_raw)

        half = SLOTS // 2
        for h in range(2):
            nc.vector.tensor_copy(tab_w[:, h * half : (h + 1) * half], tab_pool_w[:].indirect(token_list[:, h * half // 16 : (h + 1) * half // 16]))

        zh = [psum.tile([P, PACK, CHUNK], F32, name=f"zh{c}") for c in range(CHUNKS)]
        c0 = psum.tile([P, SLOTS], F32, name="c0")
        scores = psum.tile([P, SLOTS], F32, name="scores")
        hs_bf = [tile(f"hs_bf{c}", [P, CHUNK, PACK], BF16)[:] for c in range(HELD)]
        hs_w = [tile(f"hs_w{c}", [P, CHUNK], U32) for c in range(CHUNKS)]
        hs_s = [tile(f"hs_s{c}", [P, CHUNK], U8) for c in range(CHUNKS)]

        def layer(c):
            cols = slice(c * CHUNK, (c + 1) * CHUNK)
            for t in range(PACK):
                feats = slice(t * P, (t + 1) * P)
                nc.tensor.matmul_mx(zh[c][:, t, :], w1_w[:, feats].bitcast(FP8X4), w1_s[:, feats], tab_w[:, cols].bitcast(FP8X4), tab_s[TAB_ROW:P, cols], start=True, stop=True)

        def gate(c):
            nc.vector.tensor_tensor(
                hs_bf[c].rearrange("p (c i) t -> p c t i", i=4),
                zh[c][:].rearrange("p t (c i) -> p c t i", i=4),
                factor[:, c * CHUNK // 4 : (c + 1) * CHUNK // 4, :, :],
                ALU.mult,
            )

        def quantize_hs(c):
            quantize(hs_w[c][:], hs_s[c][:], hs_bf[c])

        def read_back(c):
            nc.tensor.matmul_mx(c0[:, c * CHUNK : (c + 1) * CHUNK], gout_w[:].bitcast(FP8X4), gout_s[:], hs_w[c][:].bitcast(FP8X4), hs_s[c][:], start=True, stop=True)

        neg_max, z, inv_z, total512 = [tile(f"stat{n}", [P, 1], F32) for n in range(4)]
        p = tile("p", [P, SLOTS], F32)
        weighted = tile("weighted", [P, SLOTS], F32)
        shift = tile("shift", [P, SLOTS], F32)
        inv_pair = tile("inv_pair", [P, 2], F32)

        for c in range(CHUNKS):
            layer(c)
        gate(0)
        gate(1)
        quantize_hs(0)
        quantize(query_w[:], query_s[:], query_bf[:])
        quantize_hs(1)
        nc.vector.tensor_copy(keys_w[:], keys_pool_w[:].indirect(token_list[:]))
        nc.tensor.matmul_mx(scores[:], query_w[:].bitcast(FP8X4), query_s[:], keys_w[:].bitcast(FP8X4), keys_s[KEYS_ROW:P, :], start=True, stop=True)
        held = pool.tile([P, 2, CHUNK, PACK], BF16, name="hs_held", tag="keys_pool_w", align_bytes=64)
        hs_bf.extend(held[:, c] for c in range(CHUNKS - HELD))
        gate(2)
        nc.vector.tensor_reduce(neg_max[:], scores[:], AXIS.X, ALU.max, negate=True)
        nc.scalar.activation(p[:], scores[:], ACT.Exp, bias=neg_max[:], accum_out=z[:])
        gate(3)
        quantize(gout_w[:], gout_s[:], gout_bf[:])
        quantize_hs(2)
        quantize_hs(3)
        for c in range(CHUNKS):
            read_back(c)

        nc.vector.reciprocal(inv_z[:], z[:])
        nc.vector.tensor_scalar(inv_pair[:], consts[:], inv_z[:], None, ALU.mult)
        nc.vector.scalar_tensor_tensor(weighted[:], c0[:], inv_pair[:, 0:1], p[:], ALU.mult, ALU.mult, accum_out=total512[:])
        nc.vector.tensor_scalar(shift[:], p[:], total512[:], inv_pair[:, 1:2], ALU.mult, ALU.mult)
        nc.vector.tensor_tensor(placed[:].indirect(token_list[:]), weighted[:], shift[:], ALU.add)

        start = 0
        for n, width in enumerate(STORE_WIDTHS):
            cols = slice(start, start + width)
            total = tile(f"total{n}", [P, width], F32)
            nc.vector.tensor_tensor(total[:], placed[:, cols], old_rows[:, cols], ALU.add)
            queue = nc.sync if n % 2 == 0 else nc.scalar
            queue.dma_start(out[:, cols], total[:])
            start = start + width
